import numpy as np
import ml_dtypes


def mxq(x, axis, fmt="e4m3"):
    dtype, down = {"e4m3": (ml_dtypes.float8_e4m3fn, 7), "e5m2": (ml_dtypes.float8_e5m2, 14)}[fmt]
    v = np.moveaxis(np.asarray(x, np.float32).astype(ml_dtypes.bfloat16).astype(np.float64), axis, -1)
    blocks = v.reshape(v.shape[:-1] + (-1, 32))
    amax = np.abs(blocks).max(-1, keepdims=True)
    byte = np.maximum(np.where(amax > 0, np.frexp(amax)[1] - 1 + 127, 0) - down, 1)
    scale = np.exp2(byte - 127.0)
    codes = (blocks / scale).astype(np.float32).astype(dtype).astype(np.float64)
    return np.moveaxis((codes * scale).reshape(v.shape), -1, axis)


WIDE = False


def mx_kscale(k):
    if not WIDE:
        return np.ones(k)
    levels = np.array([30, -30])
    if k % 512:
        return np.exp2(np.random.permutation(np.resize(levels, k // 32))).repeat(32)
    a = np.empty((k // 512, 16))
    for p in range(k // 512):
        a[p, :8] = np.random.permutation(np.resize(levels, 8))
        for g in range(8):
            far = levels[np.abs(levels - a[p, g]) >= 10]
            a[p, g + 8] = far[np.random.randint(len(far))]
    return np.exp2(a.ravel()).repeat(32)


def f64(x):
    return np.asarray(x).astype(np.float64)


def striped(idx):
    return np.tile(np.asarray(idx).reshape(-1, 16).T, (8, 1)).astype(np.uint16)


def unstriped(offs):
    return offs[:16].T.reshape(-1).astype(np.int64)


E2M1 = np.array([0.0, 0.5, 1.0, 1.5, 2.0, 3.0, 4.0, 6.0, -0.0, -0.5, -1.0, -1.5, -2.0, -3.0, -4.0, -6.0])


def pack_weight(w, fmt):
    k, n = w.shape
    w = f64(np.asarray(w, np.float32).astype(ml_dtypes.bfloat16)).reshape(k // 32, 32, n)
    amax = np.abs(w).max(1)
    if fmt in ("e4m3", "e5m2"):
        byte = np.frexp(amax)[1] - 1 + 127 - (7 if fmt == "e4m3" else 14)
    else:
        mant, ex = np.frexp(amax / 6.0)
        byte = np.where(mant > 0.5, ex, ex - 1) + 127
    byte = np.clip(np.where(amax > 0, byte, 1), 1, 254)
    scaled = (w * np.exp2(127.0 - byte)[:, None, :]).reshape(k, n).astype(np.float32)
    by_word = np.ascontiguousarray(scaled.reshape(k // 512, 128, 4, n).transpose(0, 1, 3, 2))
    if fmt in ("e4m3", "e5m2"):
        words = by_word.astype(ml_dtypes.float8_e4m3fn if fmt == "e4m3" else ml_dtypes.float8_e5m2).view(np.uint8)
    else:
        c = by_word.astype(ml_dtypes.float4_e2m1fn).view(np.uint8) & 0xF
        words = (c[..., 0::2] | (c[..., 1::2] << 4)).reshape(k // 512, 128, 2 * n)
    return np.ascontiguousarray(words), np.ascontiguousarray(byte.astype(np.uint8).reshape(k // 512, 16, n))


def unpack_weight(words, scales, fmt):
    g, _, n = scales.shape
    words = np.ascontiguousarray(words).reshape(g, 128, n, -1)
    if fmt in ("e4m3", "e5m2"):
        vals = words.view(ml_dtypes.float8_e4m3fn if fmt == "e4m3" else ml_dtypes.float8_e5m2).astype(np.float64)
    else:
        nib = np.empty((g, 128, n, 4), np.uint8)
        nib[..., 0::2] = words & 0xF
        nib[..., 1::2] = words >> 4
        vals = E2M1[nib]
    vals = vals * np.repeat(np.exp2(scales.astype(np.float64) - 127.0), 8, axis=1)[..., None]
    return vals.transpose(0, 1, 3, 2).reshape(g * 512, n)


def sigmoid(v):
    return 1.0 / (1.0 + np.exp(-v))


K, T, J, R, C, O, N, E = 512, 1024, 256, 512, 512, 128, 256, 512


def setup_inputs():
    n = np.random.standard_normal
    idx = np.random.permutation(T)[:J]
    idx2 = np.random.permutation(C)[:J]
    idx3 = np.random.permutation(C)[:O]
    idx4 = np.random.permutation(C)[:O]
    idx5 = np.random.permutation(J)[:O]
    idx6 = np.random.permutation(E)[:O]
    idx7 = np.random.permutation(E)[:O]
    fk = mx_kscale(K)
    fr = mx_kscale(R)
    xtp = pack_weight(n((K, T)) / fk[:, None], "e2m1")
    wp = pack_weight(n((K, R)) * 1 / np.sqrt(K) * fk[:, None], "e5m2")
    w2p = pack_weight(n((K, R)) * 1 / np.sqrt(K) * fk[:, None], "e4m3")
    wbp = pack_weight(n((R, N)) * 1 / np.sqrt(R) / fr[:, None], "e4m3")
    return {
        "xt_words": xtp[0],
        "xt_scales": xtp[1],
        "w_words": wp[0],
        "w_scales": wp[1],
        "w2_words": w2p[0],
        "w2_scales": w2p[1],
        "sa": (np.random.uniform(0.5, 1.6, (R, 1)) * fr[:, None]).astype(np.float32),
        "sb": (np.random.uniform(0.5, 1.6, (R, 1)) * fr[:, None]).astype(np.float32),
        "bg": (np.random.uniform(-2.0, 2.0, (R, 1))).astype(np.float32),
        "wb_words": wbp[0],
        "wb_scales": wbp[1],
        "offs": striped(idx),
        "offs2": striped(idx2),
        "offs3": striped(idx3),
        "offs4": striped(idx4),
        "offs5": striped(idx5),
        "offs6": striped(idx6),
        "offs7": striped(idx7),
    }


def reference(xt_words, xt_scales, w_words, w_scales, w2_words, w2_scales, sa, sb, bg, wb_words, wb_scales, offs, offs2, offs3, offs4, offs5, offs6, offs7):
    idx = unstriped(offs)
    idx2 = unstriped(offs2)
    idx3 = unstriped(offs3)
    idx4 = unstriped(offs4)
    idx5 = unstriped(offs5)
    idx6 = unstriped(offs6)
    idx7 = unstriped(offs7)
    xtu = unpack_weight(xt_words, xt_scales, "e2m1")
    wu = unpack_weight(w_words, w_scales, "e5m2")
    w2u = unpack_weight(w2_words, w2_scales, "e4m3")
    wbu = unpack_weight(wb_words, wb_scales, "e4m3")
    xtidxg = xtu[:, idx]
    a = wu.T @ xtidxg
    b = w2u.T @ xtidxg
    lb = b[:, 0:1]
    pw = np.zeros((R, C))
    pw[:, idx2] = a
    u1 = pw[:, idx3] * f64(sa) * sigmoid(pw[:, idx4] * lb + f64(bg))
    hid = np.abs(u1 - b[:, idx5] * f64(sb))
    hidq = mxq(hid, 0, "e5m2")
    p = wbu.T @ hidq
    pa = np.zeros((N, E))
    pa[:, idx6] = p
    pb = np.zeros((N, E))
    pb[:, idx7] = p
    y = pa + pb
    return y

@@ -1,0 +1,199 @@
+from contextlib import ExitStack
+
+import concourse.mybir as mybir
+
+K, T, J, R, C, O, N, E = 512, 1024, 256, 512, 512, 128, 256, 512
+FLOPS = 2 * K * R * J * 2 + 2 * R * N * O
+
+F32 = mybir.dt.float32
+BF16 = mybir.dt.bfloat16
+I32 = mybir.dt.int32
+U32 = mybir.dt.uint32
+U16 = mybir.dt.uint16
+U8 = mybir.dt.uint8
+E2M1 = mybir.dt.float4_e2m1fn_x4
+E4M3 = mybir.dt.float8_e4m3fn_x4
+E5M2 = mybir.dt.float8_e5m2_x4
+ACT = mybir.ActivationFunctionType
+ALU = mybir.AluOpType
+
+P = 128
+PACK = 4
+QUADS = 4
+QUAD = 32
+
+
+def tile_list_slopeboard_twow_one_pagetwice_kernel(
+    tc, xt_words, xt_scales, w_words, w_scales, w2_words, w2_scales, sa, sb, bg, wb_words, wb_scales,
+    offs, offs2, offs3, offs4, offs5, offs6, offs7, out,
+):
+    nc = tc.nc
+    with ExitStack() as ctx:
+        lists = ctx.enter_context(tc.tile_pool(name="lists", bufs=1))
+        pool = ctx.enter_context(tc.tile_pool(name="work", bufs=1))
+        shared = ctx.enter_context(tc.tile_pool(name="shared", bufs=1))
+        psum = ctx.enter_context(tc.psum_pool(name="psum", bufs=1))
+
+        def sb_tile(shape, dtype, name, tag=None):
+            return pool.tile(shape, dtype, name=name, tag=tag or name, align_bytes=64)
+
+        def shared_tile(shape, dtype, name, offset):
+            return shared.tile(shape, dtype, name=name, align_bytes=64, offset=offset)
+
+        def load_list(src, name):
+            t = lists.tile(list(src.shape), U16, name=name)
+            nc.sync.dma_start(t[:], src)
+            return t
+
+        def load_plane(plane, scales):
+            for q in range(QUADS):
+                nc.sync.dma_start(plane[QUAD * q : QUAD * q + 4, :].bitcast(I32), scales[0, 4 * q : 4 * q + 4, :].bitcast(I32))
+
+        def load_column(src, name):
+            t = sb_tile([P, PACK], F32, name)
+            nc.sync.dma_start(t[:], src.rearrange("(p t) o -> p (t o)", t=PACK))
+            return t
+
+        def words_of(src):
+            return src[0].rearrange("p n t -> p (n t)").bitcast(I32)
+
+        x_plane = sb_tile([P, T], U8, "x_plane")
+        w_plane_raw = sb_tile([P, R], U8, "w_plane_raw")
+        w2_plane_raw = shared_tile([P, R], U8, "w2_plane_raw", 2048)
+        wb_plane = sb_tile([P, N], U8, "wb_plane")
+        for t in (x_plane, w2_plane_raw, w_plane_raw, wb_plane):
+            nc.vector.memset(t[:].bitcast(I32), 0)
+        board = [sb_tile([P, C], F32, "board%d" % i) for i in range(PACK)]
+        for i in range(PACK):
+            nc.vector.memset(board[i][:], 0.0)
+
+        w_stage = sb_tile([4, QUADS, R // 4], I32, "w_stage")
+        nc.scalar.dma_start(w_stage[:], w_scales[0].rearrange("(q r) c -> r q c", q=QUADS).bitcast(I32))
+        l1 = load_list(offs, "l1")
+        load_plane(x_plane, xt_scales)
+        x_words = shared_tile([P, T], U16, "x_words", 0)
+        nc.scalar.dma_start(x_words[:].bitcast(I32), xt_words[0].bitcast(I32))
+        w_raw = sb_tile([P, R], U32, "w_raw")
+        nc.scalar.dma_start(w_raw[:].bitcast(I32), words_of(w_words))
+        w2_raw = shared_tile([P, R], U32, "w2_raw", 10240 + 512)
+        nc.sync.dma_start(w2_raw[:].bitcast(I32), words_of(w2_words))
+        load_plane(w2_plane_raw, w2_scales)
+        l2 = load_list(offs2, "l2")
+        l3 = load_list(offs3, "l3")
+        sa_t = load_column(sa, "sa_t")
+        l5 = load_list(offs5, "l5")
+        sb_t = load_column(sb, "sb_t")
+        l4 = load_list(offs4, "l4")
+        bg_t = load_column(bg, "bg_t")
+        wb = sb_tile([P, N], U32, "wb")
+        nc.sync.dma_start(wb[:].bitcast(I32), words_of(wb_words))
+        load_plane(wb_plane, wb_scales)
+        l6 = load_list(offs6, "l6")
+        l7 = load_list(offs7, "l7")
+
+        for q in range(QUADS):
+            nc.vector.tensor_copy(w_plane_raw[QUAD * q : QUAD * q + 4, :].bitcast(I32), w_stage[:, q, :])
+        w_plane = sb_tile([P, PACK, P], U8, "w_plane")
+        nc.vector.tensor_copy(w_plane[:], w_plane_raw[:].rearrange("p (m i) -> p i m", i=PACK))
+        xg_plane = sb_tile([P, J], U8, "xg_plane")
+        nc.vector.tensor_copy(xg_plane[:], x_plane[:].indirect(l1[:]))
+        xg = sb_tile([P, J], U16, "xg")
+        nc.vector.tensor_copy(xg[:], x_words[:].indirect(l1[:]))
+
+        w_dealt = [sb_tile([P, P], U32, "w_dealt%d" % i) for i in range(PACK)]
+        for i in range(PACK):
+            nc.scalar.copy(w_dealt[i][:], w_raw[:].rearrange("p (m i) -> p i m", i=PACK)[:, i, :])
+        def first_product(i, bank):
+            acc = psum.tile([P, J], F32, name="a_ps%d" % i, tag="bank%d" % bank)
+            nc.tensor.matmul_mx(
+                out=acc[:], lhsT=w_dealt[i][:].bitcast(E5M2), lhsT_scale=w_plane[:, i, :],
+                rhs=xg[:].bitcast(E2M1), rhs_scale=xg_plane[:], start=True, stop=True,
+            )
+            return acc
+
+        a_ps = [first_product(i, i) for i in range(PACK)]
+
+        w2_plane = shared_tile([P, PACK, P], U8, "w2_plane", 0)
+        nc.vector.tensor_copy(w2_plane[:], w2_plane_raw[:].rearrange("p (m i) -> p i m", i=PACK))
+        w2_dealt = shared_tile([P, PACK, P], U32, "w2_dealt", 512)
+        nc.vector.tensor_copy(w2_dealt[:].bitcast(I32), w2_raw[:].bitcast(I32).rearrange("p (m i) -> p i m", i=PACK))
+        b_ps = [psum.tile([P, J], F32, name="b_ps%d" % i, tag="bank%d" % (PACK + i)) for i in range(PACK)]
+        for i in range(PACK):
+            nc.tensor.matmul_mx(
+                out=b_ps[i][:], lhsT=w2_dealt[:, i, :].bitcast(E4M3), lhsT_scale=w2_plane[:, i, :],
+                rhs=xg[:].bitcast(E2M1), rhs_scale=xg_plane[:], start=True, stop=True,
+            )
+
+        a_sb = [sb_tile([P, J], F32, "a_sb0")] + [shared_tile([P, J], F32, "a_sb%d" % i, 10240 + 1024 * (i - 1)) for i in range(1, PACK)]
+        b_sb = [shared_tile([P, J], F32, "b_sb%d" % i, 4096 + 1024 * i) for i in range(PACK)]
+        gate = [sb_tile([P, O], F32, "gate%d" % i) for i in range(3)] + [shared_tile([P, O], F32, "gate3", 4096 + 2048)]
+        first = [sb_tile([P, O], F32, "first%d" % i) for i in range(2)]
+        first.append(shared_tile([P, O], F32, "first2", 4096 + 1024))
+        first.append(shared_tile([P, O], F32, "first3", 4096 + 2048 + 512))
+        second = sb_tile([P, PACK, O], F32, "second")
+        prod = sb_tile([P, PACK, O], F32, "prod")
+        diff = sb_tile([P, PACK, O], F32, "diff")
+
+        def fetch_second(i):
+            nc.scalar.activation(second[:, i, :], b_sb[i][:].indirect(l5[:]), ACT.Copy, scale=sb_t[:, i : i + 1])
+
+        def fetch_gate(i):
+            nc.scalar.activation(gate[i][:], board[i][:].indirect(l4[:]), ACT.Sigmoid, bias=bg_t[:, i : i + 1], scale=b_sb[i][:, 0:1])
+
+        def fetch_first(i):
+            nc.scalar.activation(first[i][:], board[i][:].indirect(l3[:]), ACT.Copy, scale=sa_t[:, i : i + 1])
+
+        def combine(i):
+            nc.vector.tensor_tensor(prod[:, i, :], first[i][:], gate[i][:], ALU.mult)
+            nc.vector.tensor_tensor(diff[:, i, :], prod[:, i, :], second[:, i, :], ALU.subtract)
+
+        nc.scalar.copy(a_sb[0][:], a_ps[0][:])
+        nc.scalar.activation(board[0][:].indirect(l2[:]), a_sb[0][:], ACT.Copy)
+        for i in range(1, PACK):
+            nc.vector.tensor_copy(a_sb[i][:], a_ps[i][:])
+            nc.vector.tensor_copy(board[i][:].indirect(l2[:]), a_sb[i][:])
+        for i in range(PACK):
+            nc.scalar.copy(b_sb[i][:], b_ps[i][:])
+        for i in range(2):
+            fetch_first(i)
+        for i in range(PACK):
+            fetch_second(i)
+        for i in range(2):
+            fetch_gate(i)
+        for i in range(2, PACK):
+            fetch_gate(i)
+            fetch_first(i)
+        for i in range(PACK):
+            combine(i)
+
+        pa = [sb_tile([P, E], F32, "pa0", tag="a_sb0"), sb_tile([P, E], F32, "pa1", tag="board0")]
+        pb = [shared_tile([P, E], F32, "pb0", 10240 - 1024), sb_tile([P, E], F32, "pb1", tag="board1")]
+        for t in (pa[0], pb[0], pa[1], pb[1]):
+            nc.gpsimd.memset(t[:], 0.0)
+
+        hid = sb_tile([P, O, PACK], BF16, "hid")
+        woven = diff[:].rearrange("p i o -> p o i")
+        nc.scalar.activation(hid[:, 0 : O // 2, :], woven[:, 0 : O // 2, :], ACT.Abs)
+        nc.vector.scalar_tensor_tensor(hid[:, O // 2 : O, :], woven[:, O // 2 : O, :], -1.0, woven[:, O // 2 : O, :], ALU.mult, ALU.max)
+        hid_words = sb_tile([P, O], U32, "hid_words")
+        hid_plane = sb_tile([P, O], U8, "hid_plane")
+        nc.vector.quantize_mx(out=hid_words[:].bitcast(E5M2), scales=hid_plane[:], in_=hid[:].rearrange("p o i -> p (o i)"))
+
+        p_ps = [psum.tile([P, O], F32, name="p_ps%d" % h, tag="bank%d" % h) for h in range(2)]
+        p_sb = [sb_tile([P, O], F32, "p_sb%d" % h) for h in range(2)]
+        res = [sb_tile([P, E], F32, "res%d" % h) for h in range(2)]
+        for h in range(2):
+            cols = slice(P * h, P * (h + 1))
+            nc.tensor.matmul_mx(
+                out=p_ps[h][:], lhsT=wb[:, cols].bitcast(E4M3), lhsT_scale=wb_plane[:, cols],
+                rhs=hid_words[:].bitcast(E5M2), rhs_scale=hid_plane[:], start=True, stop=True,
+            )
+        nc.vector.tensor_copy(p_sb[0][:], p_ps[0][:])
+        nc.scalar.copy(p_sb[1][:], p_ps[1][:])
+        nc.vector.tensor_copy(pa[0][:].indirect(l6[:]), p_sb[0][:])
+        nc.scalar.activation(pb[0][:].indirect(l7[:]), p_sb[0][:], ACT.Copy)
+        nc.vector.tensor_copy(pa[1][:].indirect(l6[:]), p_sb[1][:])
+        nc.scalar.activation(pb[1][:].indirect(l7[:]), p_sb[1][:], ACT.Copy)
+        for h in range(2):
+            nc.vector.tensor_tensor(res[h][:], pa[h][:], pb[h][:], ALU.add)
+            nc.sync.dma_start(out[P * h : P * (h + 1), :], res[h][:])

@@ -100,6 +100,9 @@ def tile_list_slopeboard_twow_one_pagetwice_kernel(
         xg = sb_tile([P, J], U16, "xg")
         nc.vector.tensor_copy(xg[:], x_words[:].indirect(l1[:]))
 
+        warm = sb_tile([P, 2], F32, "warm")
+        nc.gpsimd.memset(warm[:, 0:1], 0.0)
+        nc.scalar.activation(warm[:, 1:2], warm[:, 0:1], ACT.Sigmoid)
         w_dealt = [sb_tile([P, P], U32, "w_dealt%d" % i) for i in range(PACK)]
         for i in range(PACK):
             nc.scalar.copy(w_dealt[i][:], w_raw[:].rearrange("p (m i) -> p i m", i=PACK)[:, i, :])

from contextlib import ExitStack

import concourse.mybir as mybir

K, T, J, R, C, O, N, E = 512, 1024, 256, 512, 512, 128, 256, 512
FLOPS = 2 * K * R * J * 2 + 2 * R * N * O

F32 = mybir.dt.float32
BF16 = mybir.dt.bfloat16
I32 = mybir.dt.int32
U32 = mybir.dt.uint32
U16 = mybir.dt.uint16
U8 = mybir.dt.uint8
E2M1 = mybir.dt.float4_e2m1fn_x4
E4M3 = mybir.dt.float8_e4m3fn_x4
E5M2 = mybir.dt.float8_e5m2_x4
ACT = mybir.ActivationFunctionType
ALU = mybir.AluOpType

P = 128
PACK = 4
QUADS = 4
QUAD = 32


def tile_list_slopeboard_twow_one_pagetwice_kernel(
    tc, xt_words, xt_scales, w_words, w_scales, w2_words, w2_scales, sa, sb, bg, wb_words, wb_scales,
    offs, offs2, offs3, offs4, offs5, offs6, offs7, out,
):
    nc = tc.nc
    with ExitStack() as ctx:
        lists = ctx.enter_context(tc.tile_pool(name="lists", bufs=1))
        pool = ctx.enter_context(tc.tile_pool(name="work", bufs=1))
        shared = ctx.enter_context(tc.tile_pool(name="shared", bufs=1))
        psum = ctx.enter_context(tc.psum_pool(name="psum", bufs=1))

        def sb_tile(shape, dtype, name, tag=None):
            return pool.tile(shape, dtype, name=name, tag=tag or name, align_bytes=64)

        def shared_tile(shape, dtype, name, offset):
            return shared.tile(shape, dtype, name=name, align_bytes=64, offset=offset)

        def load_list(src, name):
            t = lists.tile(list(src.shape), U16, name=name)
            nc.sync.dma_start(t[:], src)
            return t

        def load_plane(plane, scales):
            for q in range(QUADS):
                nc.sync.dma_start(plane[QUAD * q : QUAD * q + 4, :].bitcast(I32), scales[0, 4 * q : 4 * q + 4, :].bitcast(I32))

        def load_column(src, name):
            t = sb_tile([P, PACK], F32, name)
            nc.sync.dma_start(t[:], src.rearrange("(p t) o -> p (t o)", t=PACK))
            return t

        def words_of(src):
            return src[0].rearrange("p n t -> p (n t)").bitcast(I32)

        x_plane = sb_tile([P, T], U8, "x_plane")
        w_plane_raw = sb_tile([P, R], U8, "w_plane_raw")
        w2_plane_raw = shared_tile([P, R], U8, "w2_plane_raw", 2048)
        wb_plane = sb_tile([P, N], U8, "wb_plane")
        for t in (x_plane, w2_plane_raw, w_plane_raw, wb_plane):
            nc.vector.memset(t[:].bitcast(I32), 0)
        board = [sb_tile([P, C], F32, "board%d" % i) for i in range(PACK)]
        for i in range(PACK):
            nc.vector.memset(board[i][:], 0.0)

        w_stage = sb_tile([4, QUADS, R // 4], I32, "w_stage")
        nc.scalar.dma_start(w_stage[:], w_scales[0].rearrange("(q r) c -> r q c", q=QUADS).bitcast(I32))
        l1 = load_list(offs, "l1")
        load_plane(x_plane, xt_scales)
        x_words = shared_tile([P, T], U16, "x_words", 0)
        nc.scalar.dma_start(x_words[:].bitcast(I32), xt_words[0].bitcast(I32))
        w_raw = sb_tile([P, R], U32, "w_raw")
        nc.scalar.dma_start(w_raw[:].bitcast(I32), words_of(w_words))
        w2_raw = shared_tile([P, R], U32, "w2_raw", 10240 + 512)
        nc.sync.dma_start(w2_raw[:].bitcast(I32), words_of(w2_words))
        load_plane(w2_plane_raw, w2_scales)
        l2 = load_list(offs2, "l2")
        l3 = load_list(offs3, "l3")
        sa_t = load_column(sa, "sa_t")
        l5 = load_list(offs5, "l5")
        sb_t = load_column(sb, "sb_t")
        l4 = load_list(offs4, "l4")
        bg_t = load_column(bg, "bg_t")
        wb = sb_tile([P, N], U32, "wb")
        nc.sync.dma_start(wb[:].bitcast(I32), words_of(wb_words))
        load_plane(wb_plane, wb_scales)
        l6 = load_list(offs6, "l6")
        l7 = load_list(offs7, "l7")

        for q in range(QUADS):
            nc.vector.tensor_copy(w_plane_raw[QUAD * q : QUAD * q + 4, :].bitcast(I32), w_stage[:, q, :])
        w_plane = sb_tile([P, PACK, P], U8, "w_plane")
        nc.vector.tensor_copy(w_plane[:], w_plane_raw[:].rearrange("p (m i) -> p i m", i=PACK))
        xg_plane = sb_tile([P, J], U8, "xg_plane")
        nc.vector.tensor_copy(xg_plane[:], x_plane[:].indirect(l1[:]))
        xg = sb_tile([P, J], U16, "xg")
        nc.vector.tensor_copy(xg[:], x_words[:].indirect(l1[:]))

        warm = sb_tile([P, 2], F32, "warm")
        nc.gpsimd.memset(warm[:, 0:1], 0.0)
        nc.scalar.activation(warm[:, 1:2], warm[:, 0:1], ACT.Sigmoid)
        w_dealt = [sb_tile([P, P], U32, "w_dealt%d" % i) for i in range(PACK)]
        for i in range(PACK):
            nc.scalar.copy(w_dealt[i][:], w_raw[:].rearrange("p (m i) -> p i m", i=PACK)[:, i, :])
        def first_product(i, bank):
            acc = psum.tile([P, J], F32, name="a_ps%d" % i, tag="bank%d" % bank)
            nc.tensor.matmul_mx(
                out=acc[:], lhsT=w_dealt[i][:].bitcast(E5M2), lhsT_scale=w_plane[:, i, :],
                rhs=xg[:].bitcast(E2M1), rhs_scale=xg_plane[:], start=True, stop=True,
            )
            return acc

        a_ps = [first_product(i, i) for i in range(PACK)]

        w2_plane = shared_tile([P, PACK, P], U8, "w2_plane", 0)
        nc.vector.tensor_copy(w2_plane[:], w2_plane_raw[:].rearrange("p (m i) -> p i m", i=PACK))
        w2_dealt = shared_tile([P, PACK, P], U32, "w2_dealt", 512)
        nc.vector.tensor_copy(w2_dealt[:].bitcast(I32), w2_raw[:].bitcast(I32).rearrange("p (m i) -> p i m", i=PACK))
        b_ps = [psum.tile([P, J], F32, name="b_ps%d" % i, tag="bank%d" % (PACK + i)) for i in range(PACK)]
        for i in range(PACK):
            nc.tensor.matmul_mx(
                out=b_ps[i][:], lhsT=w2_dealt[:, i, :].bitcast(E4M3), lhsT_scale=w2_plane[:, i, :],
                rhs=xg[:].bitcast(E2M1), rhs_scale=xg_plane[:], start=True, stop=True,
            )

        a_sb = [sb_tile([P, J], F32, "a_sb0")] + [shared_tile([P, J], F32, "a_sb%d" % i, 10240 + 1024 * (i - 1)) for i in range(1, PACK)]
        b_sb = [shared_tile([P, J], F32, "b_sb%d" % i, 4096 + 1024 * i) for i in range(PACK)]
        gate = [sb_tile([P, O], F32, "gate%d" % i) for i in range(3)] + [shared_tile([P, O], F32, "gate3", 4096 + 2048)]
        first = [sb_tile([P, O], F32, "first%d" % i) for i in range(2)]
        first.append(shared_tile([P, O], F32, "first2", 4096 + 1024))
        first.append(shared_tile([P, O], F32, "first3", 4096 + 2048 + 512))
        second = sb_tile([P, PACK, O], F32, "second")
        prod = sb_tile([P, PACK, O], F32, "prod")
        diff = sb_tile([P, PACK, O], F32, "diff")

        def fetch_second(i):
            nc.scalar.activation(second[:, i, :], b_sb[i][:].indirect(l5[:]), ACT.Copy, scale=sb_t[:, i : i + 1])

        def fetch_gate(i):
            nc.scalar.activation(gate[i][:], board[i][:].indirect(l4[:]), ACT.Sigmoid, bias=bg_t[:, i : i + 1], scale=b_sb[i][:, 0:1])

        def fetch_first(i):
            nc.scalar.activation(first[i][:], board[i][:].indirect(l3[:]), ACT.Copy, scale=sa_t[:, i : i + 1])

        def combine(i):
            nc.vector.tensor_tensor(prod[:, i, :], first[i][:], gate[i][:], ALU.mult)
            nc.vector.tensor_tensor(diff[:, i, :], prod[:, i, :], second[:, i, :], ALU.subtract)

        nc.scalar.copy(a_sb[0][:], a_ps[0][:])
        nc.scalar.activation(board[0][:].indirect(l2[:]), a_sb[0][:], ACT.Copy)
        for i in range(1, PACK):
            nc.vector.tensor_copy(a_sb[i][:], a_ps[i][:])
            nc.vector.tensor_copy(board[i][:].indirect(l2[:]), a_sb[i][:])
        for i in range(PACK):
            nc.scalar.copy(b_sb[i][:], b_ps[i][:])
        for i in range(2):
            fetch_first(i)
        for i in range(PACK):
            fetch_second(i)
        for i in range(2):
            fetch_gate(i)
        for i in range(2, PACK):
            fetch_gate(i)
            fetch_first(i)
        for i in range(PACK):
            combine(i)

        pa = [sb_tile([P, E], F32, "pa0", tag="a_sb0"), sb_tile([P, E], F32, "pa1", tag="board0")]
        pb = [shared_tile([P, E], F32, "pb0", 10240 - 1024), sb_tile([P, E], F32, "pb1", tag="board1")]
        for t in (pa[0], pb[0], pa[1], pb[1]):
            nc.gpsimd.memset(t[:], 0.0)

        hid = sb_tile([P, O, PACK], BF16, "hid")
        woven = diff[:].rearrange("p i o -> p o i")
        nc.scalar.activation(hid[:, 0 : O // 2, :], woven[:, 0 : O // 2, :], ACT.Abs)
        nc.vector.scalar_tensor_tensor(hid[:, O // 2 : O, :], woven[:, O // 2 : O, :], -1.0, woven[:, O // 2 : O, :], ALU.mult, ALU.max)
        hid_words = sb_tile([P, O], U32, "hid_words")
        hid_plane = sb_tile([P, O], U8, "hid_plane")
        nc.vector.quantize_mx(out=hid_words[:].bitcast(E5M2), scales=hid_plane[:], in_=hid[:].rearrange("p o i -> p (o i)"))

        p_ps = [psum.tile([P, O], F32, name="p_ps%d" % h, tag="bank%d" % h) for h in range(2)]
        p_sb = [sb_tile([P, O], F32, "p_sb%d" % h) for h in range(2)]
        res = [sb_tile([P, E], F32, "res%d" % h) for h in range(2)]
        for h in range(2):
            cols = slice(P * h, P * (h + 1))
            nc.tensor.matmul_mx(
                out=p_ps[h][:], lhsT=wb[:, cols].bitcast(E4M3), lhsT_scale=wb_plane[:, cols],
                rhs=hid_words[:].bitcast(E5M2), rhs_scale=hid_plane[:], start=True, stop=True,
            )
        nc.vector.tensor_copy(p_sb[0][:], p_ps[0][:])
        nc.scalar.copy(p_sb[1][:], p_ps[1][:])
        nc.vector.tensor_copy(pa[0][:].indirect(l6[:]), p_sb[0][:])
        nc.scalar.activation(pb[0][:].indirect(l7[:]), p_sb[0][:], ACT.Copy)
        nc.vector.tensor_copy(pa[1][:].indirect(l6[:]), p_sb[1][:])
        nc.scalar.activation(pb[1][:].indirect(l7[:]), p_sb[1][:], ACT.Copy)
        for h in range(2):
            nc.vector.tensor_tensor(res[h][:], pa[h][:], pb[h][:], ALU.add)
            nc.sync.dma_start(out[P * h : P * (h + 1), :], res[h][:])
